import numpy as np
import ml_dtypes


def mxq(x, axis, fmt="e4m3"):
    dtype, down = {"e4m3": (ml_dtypes.float8_e4m3fn, 7), "e5m2": (ml_dtypes.float8_e5m2, 14)}[fmt]
    v = np.moveaxis(np.asarray(x, np.float32).astype(ml_dtypes.bfloat16).astype(np.float64), axis, -1)
    blocks = v.reshape(v.shape[:-1] + (-1, 32))
    amax = np.abs(blocks).max(-1, keepdims=True)
    byte = np.maximum(np.where(amax > 0, np.frexp(amax)[1] - 1 + 127, 0) - down, 1)
    scale = np.exp2(byte - 127.0)
    codes = (blocks / scale).astype(np.float32).astype(dtype).astype(np.float64)
    return np.moveaxis((codes * scale).reshape(v.shape), -1, axis)


WIDE = False


def mx_kscale(k):
    if not WIDE:
        return np.ones(k)
    levels = np.array([10, -10, 5, -5, 0])
    if k % 512:
        return np.exp2(np.random.permutation(np.resize(levels, k // 32))).repeat(32)
    a = np.empty((k // 512, 16))
    for p in range(k // 512):
        a[p, :8] = np.random.permutation(np.resize(levels, 8))
        for g in range(8):
            far = levels[np.abs(levels - a[p, g]) >= 10]
            a[p, g + 8] = far[np.random.randint(len(far))]
    return np.exp2(a.ravel()).repeat(32)


def f64(x):
    return np.asarray(x).astype(np.float64)


def striped(idx):
    return np.tile(idx.reshape(-1, 16).T, (8, 1)).astype(np.uint16)


def unstriped(offs):
    return offs[:16].T.reshape(-1).astype(np.int64)


def pack_weight(w):
    k, n = w.shape
    w = f64(np.asarray(w, np.float32).astype(ml_dtypes.bfloat16)).reshape(k // 32, 32, n)
    amax = np.abs(w).max(1)
    byte = np.clip(np.where(amax > 0, np.frexp(amax)[1] - 1 + 127 - 7, 1), 1, 254)
    scaled = (w * np.exp2(127.0 - byte)[:, None, :]).reshape(k, n).astype(np.float32)
    words = np.ascontiguousarray(scaled.reshape(k // 512, 128, 4, n).transpose(0, 1, 3, 2)).astype(ml_dtypes.float8_e4m3fn).view(np.uint8)
    return words, np.ascontiguousarray(byte.astype(np.uint8).reshape(k // 512, 16, n))


def unpack_weight(words, scales):
    g, p, n, _ = words.shape
    vals = np.ascontiguousarray(words).view(ml_dtypes.float8_e4m3fn).astype(np.float64) * np.repeat(np.exp2(scales.astype(np.float64) - 127.0), 8, axis=1)[..., None]
    return vals.transpose(0, 1, 3, 2).reshape(g * 512, n)


K, T, S, V = 1024, 2048, 512, 512
P = 2 ** 7


def setup_inputs():
    n = np.random.standard_normal
    s = mx_kscale(K)[:, None]
    packed_xT = pack_weight(n((K, T)) * s)
    return {
        "x_words": packed_xT[0],
        "x_scales": packed_xT[1],
        "hT": (n((K, V)) / np.sqrt(K) / s).astype(np.float32),
        "nn": (np.tile(np.random.uniform(0.5, 2.0, T), (P, 1))).astype(np.float32),
        "own": (np.random.uniform(0.5, 1.5, (V, 1))).astype(np.float32),
        "isc": (np.tile(np.random.uniform(0.3, 0.9, T), (P, 1))).astype(np.float32),
        "shp": (np.tile(np.random.uniform(0.8, 2.5, T), (P, 1))).astype(np.float32),
        "offs": striped(np.random.permutation(T)[:S]),
    }


def reference(x_words, x_scales, hT, nn, own, isc, shp, offs):
    hTq = mxq(f64(hT), 0, "e4m3")
    xq = unpack_weight(x_words, x_scales)[:, unstriped(offs)]
    y = hTq.T @ xq
    dis = np.log(np.exp(f64(nn)[:1][:, unstriped(offs)] - y + f64(own)) + 1.0) + 0.1
    keep = np.exp(-1.0 * (np.exp((f64(shp)[:1][:, unstriped(offs)]) * (np.log(dis * (f64(isc)[:1][:, unstriped(offs)]))))))
    yr = y * keep
    yu = np.abs(y) * (-1.0 * keep + 1.0)
    unk = yu.mean(axis=1, keepdims=True)
    return yr - unk

from contextlib import ExitStack

import concourse.mybir as mybir
from concourse.masks import make_identity

K, T, S, V = 1024, 2048, 512, 512
P = 128
PACK = 4
K_PASS = P * PACK
PASSES = K // K_PASS
TILES = V // P
HALF = V // 2

FLOPS = 2 * K * V * S
BYTES = K * T + K * T // 32 + 4 * K * V + 3 * 4 * T + 4 * V + 2 * P * S // 16 + 4 * V * S

F32 = mybir.dt.float32
BF16 = mybir.dt.bfloat16
I32 = mybir.dt.int32
U32 = mybir.dt.uint32
U16 = mybir.dt.uint16
U8 = mybir.dt.uint8
FP8X4 = mybir.dt.float8_e4m3fn_x4
ALU = mybir.AluOpType
ACT = mybir.ActivationFunctionType

SPLIT = 1280
EXP_CAP = 2.0**60


def tile_picked_yopenm_rev_p_kernel(
    tc, x_words, x_scales, hT, nn, own, isc, shp, offs, out
):
    nc = tc.nc
    with ExitStack() as ctx:
        sb = ctx.enter_context(tc.tile_pool(name="sb", bufs=1))
        ps = ctx.enter_context(tc.psum_pool(name="ps", bufs=1))

        offsets = sb.tile([P, S // 16], U16, name="offsets")
        words = [sb.tile([P, T], I32, name=f"words{g}") for g in range(PASSES)]
        scale_rows = sb.tile([P, T], U8, name="scale_rows")
        class_rows = sb.tile([P, T], F32, name="class_rows")
        own_rows = sb.tile([P, P], F32, name="own_rows")
        ident = sb.tile([P, P], F32, name="ident")

        nc.gpsimd.memset(class_rows[:, 0:SPLIT], 0.0)
        nc.vector.memset(class_rows[:, SPLIT:T], 0.0)
        nc.gpsimd.memset(own_rows[:], 0.0)
        nc.vector.memset(scale_rows[:].bitcast(I32), 0)
        make_identity(nc, ident[:])

        pieces = [(0, 0, 512), (1, 0, 256), (1, 256, 384), (1, 384, 512)]
        raw = {}

        def load_words(g):
            nc.sync.dma_start(words[g][:], x_words[g].rearrange("p n t -> p (n t)").bitcast(I32))

        for g, lo, hi in pieces:
            raw[g, lo, hi] = sb.tile([P, PACK, hi - lo], F32, name=f"raw{g}_{lo}", tag=f"raw{g}_{lo}")

        def load_h(piece, j0=0, j1=PACK):
            g, lo, hi = piece
            rows = hT[g * K_PASS : (g + 1) * K_PASS, lo:hi]
            nc.sync.dma_start(raw[piece][:, j0:j1, :], rows.rearrange("(p j) w -> p j w", j=PACK)[:, j0:j1, :])

        def load_scales(q):
            nc.sync.dma_start(
                scale_rows[32 * q : 32 * q + 8, :].bitcast(I32), x_scales[:, 4 * q : 4 * q + 4, :].bitcast(I32)
            )

        load_h(pieces[0], 0, 2)
        nc.sync.dma_start(offsets[:], offs)
        for r, row in enumerate((nn, isc, shp)):
            nc.sync.dma_start(class_rows[r : r + 1, :], row[0:1, :])
        load_scales(0)
        load_scales(1)
        load_words(0)
        load_scales(2)
        load_scales(3)
        load_h(pieces[0], 2, 4)
        nc.sync.dma_start(own_rows[0:TILES, :], own.rearrange("(c p) o -> c (p o)", p=P))
        load_words(1)
        for piece in pieces[1:]:
            load_h(piece)

        picked = [sb.tile([P, S], U32, name=f"picked{g}", align_bytes=64) for g in range(PASSES)]
        picked_scales = sb.tile([P, S], U8, name="picked_scales", align_bytes=64)
        picked_rows = sb.tile([P, S], F32, name="picked_rows")
        nc.vector.tensor_copy(picked_rows[:], class_rows[:].indirect(offsets[:]))
        nc.vector.tensor_copy(picked[0][:], words[0][:].bitcast(U32).indirect(offsets[:]))
        nc.vector.tensor_copy(picked_scales[:], scale_rows[:].indirect(offsets[:]))

        turned = ps.tile([P, TILES, P], F32, name="turned", tag="w0")
        for c in range(TILES):
            nc.tensor.transpose(turned[:, c, :], picked_rows[:, c * P : (c + 1) * P], ident[:])
        class_cols = sb.tile([P, TILES, 3], F32, name="class_cols")
        nc.scalar.copy(class_cols[:], turned[:, :, 0:3])
        own_turned = ps.tile([P, P], F32, name="own_turned", tag="w1")
        nc.tensor.transpose(own_turned[:], own_rows[:], ident[:])
        own_cols = sb.tile([P, TILES], F32, name="own_cols")
        nc.scalar.copy(own_cols[:], own_turned[:, 0:TILES])
        nn_spread = ps.tile([P, TILES, P], F32, name="nn_spread", tag="w2")
        for c in range(TILES):
            nc.tensor.transpose(nn_spread[:, c, :], class_cols[:, c, 0:1].to_broadcast([P, P]), ident[:])
        shp_row = ps.tile([P, S], F32, name="shp_row", tag="w3")
        for c in range(TILES):
            nc.tensor.transpose(shp_row[:, c * P : (c + 1) * P], class_cols[:, c, 2:3].to_broadcast([P, P]), ident[:])

        y = [ps.tile([P, S], F32, name=f"y{t}") for t in range(TILES)]
        e = sb.tile([P, TILES, S], F32, name="e", tag="e")

        def cast(engine, piece, t):
            g, lo, hi = piece
            grouped = sb.tile([P, P, PACK], BF16, name=f"grouped{g}_{t}", tag=f"grouped{g}_{t}", align_bytes=64)
            src = raw[piece][:, :, t * P - lo : (t + 1) * P - lo].rearrange("p j (c i) -> p c j i", i=4)
            dst = grouped[:].rearrange("p (c i) j -> p c j i", i=4)
            if engine == "scalar":
                nc.scalar.copy(dst, src)
            else:
                nc.vector.tensor_copy(dst, src)
            return grouped

        def quantise_multiply(g, t, grouped):
            codes = sb.tile([P, P], U32, name=f"codes{g}_{t}", align_bytes=64)
            scales = sb.tile([P, P], U8, name=f"scales{g}_{t}", align_bytes=64)
            nc.vector.quantize_mx(
                out=codes[:].bitcast(FP8X4), scales=scales[:], in_=grouped[:].rearrange("p w j -> p (w j)")
            )
            nc.tensor.matmul_mx(
                out=y[t][:],
                lhsT=codes[:].bitcast(FP8X4),
                lhsT_scale=scales[:],
                rhs=picked[g][:].bitcast(FP8X4),
                rhs_scale=picked_scales[4 * g : P, :],
                start=(g == 0),
                stop=(g == PASSES - 1),
            )

        first = [cast("scalar" if t < 3 else "vector", pieces[0], t) for t in range(TILES)]
        nn_row = sb.tile([P, S], F32, name="nn_row", tag="raw0_0")
        nc.scalar.copy(nn_row[:], nn_spread[:].rearrange("p c j -> p (c j)"))
        for t in range(TILES):
            quantise_multiply(0, t, first[t])
        nc.vector.tensor_copy(picked[1][:], words[1][:].bitcast(U32).indirect(offsets[:]))
        piece_of = [pieces[1], pieces[1], pieces[2], pieces[3]]
        for t in range(TILES):
            grouped = cast("scalar" if t in (1, 2) else "vector", piece_of[t], t)
            quantise_multiply(1, t, grouped)
        u = [
            sb.tile([P, S], F32, name=f"u{t}", tag="grouped1_3" if t == 0 else f"u{t}", align_bytes=64)
            for t in range(TILES)
        ]
        for t in range(TILES):
            nc.vector.scalar_tensor_tensor(
                u[t][:], nn_row[:], own_cols[:, t : t + 1], y[t][:], ALU.add, ALU.subtract
            )
            nc.scalar.activation(e[:, t, :], u[t][:], ACT.Exp)
        capped = sb.tile([P, TILES, S], F32, name="capped")
        nc.vector.tensor_scalar(capped[:], e[:], EXP_CAP, None, ALU.min)

        log_isc = sb.tile([P, TILES], F32, name="log_isc", tag="e")
        soft = [sb.tile([P, S], F32, name=f"soft{t}") for t in range(TILES)]
        for t in range(TILES):
            nc.scalar.activation(soft[t][:], capped[:, t, :], ACT.Ln, bias=1.0)
            if t == 0:
                nc.scalar.activation(log_isc[:], class_cols[:, :, 1], ACT.Ln)
            nc.vector.tensor_tensor(soft[t][:], soft[t][:], u[t][:], ALU.max)
        log_isc_row = ps.tile([P, S], F32, name="log_isc_row", tag="w0")
        for c in range(TILES):
            nc.tensor.transpose(log_isc_row[:, c * P : (c + 1) * P], log_isc[:, c : c + 1].to_broadcast([P, P]), ident[:])
        z = [sb.tile([P, S], F32, name=f"z{t}") for t in range(TILES)]
        for t in range(TILES):
            nc.scalar.activation(z[t][:], soft[t][:], ACT.Ln, bias=0.1)
        for t in range(TILES + 1):
            if t < TILES:
                nc.vector.tensor_tensor(z[t][:], z[t][:], log_isc_row[:], ALU.add)
            if t > 0:
                nc.vector.tensor_tensor(z[t - 1][:], z[t - 1][:], shp_row[:], ALU.mult)

        keep = [sb.tile([P, S], F32, name=f"keep{t}") for t in range(TILES)]
        taken = [sb.tile([P, S], F32, name=f"taken{t}") for t in range(TILES)]
        unk = [sb.tile([P, 1], F32, name=f"unk{t}") for t in range(TILES)]

        def survive(t):
            nc.scalar.activation(z[t][:], z[t][:], ACT.Exp)
            nc.scalar.activation(keep[t][:], z[t][:], ACT.Exp, scale=-1.0)
            nc.vector.scalar_tensor_tensor(taken[t][:], keep[t][:], 1.0, y[t][:], ALU.subtract, ALU.mult)

        def mean_on_vector(t):
            total = sb.tile([P, 1], F32, name=f"total{t}")
            nc.vector.tensor_reduce(total[:], taken[t][:], mybir.AxisListType.X, ALU.add, apply_absolute_value=True)
            nc.vector.tensor_scalar(unk[t][:], total[:], 1.0 / S, None, ALU.mult)

        def mean_on_scalar(t):
            nc.scalar.activation(keep[t][:], taken[t][:], ACT.Abs, scale=1.0 / S, accum_out=unk[t][:])

        def finish(t):
            result = sb.tile([P, S], F32, name=f"result{t}")
            nc.vector.scalar_tensor_tensor(result[:], taken[t][:], unk[t][:], y[t][:], ALU.subtract, ALU.add)
            nc.sync.dma_start(out[t * P : (t + 1) * P, :], result[:])

        survive(0)
        mean_on_vector(0)
        survive(1)
        finish(0)
        mean_on_vector(1)
        survive(2)
        survive(3)
        finish(1)
        mean_on_scalar(2)
        mean_on_scalar(3)
        finish(2)
        finish(3)
